import numpy as np
import ml_dtypes


def mxq(x, axis, fmt="e4m3"):
    dtype, down = {"e4m3": (ml_dtypes.float8_e4m3fn, 7), "e5m2": (ml_dtypes.float8_e5m2, 14)}[fmt]
    v = np.moveaxis(np.asarray(x, np.float32).astype(ml_dtypes.bfloat16).astype(np.float64), axis, -1)
    blocks = v.reshape(v.shape[:-1] + (-1, 32))
    amax = np.abs(blocks).max(-1, keepdims=True)
    byte = np.maximum(np.where(amax > 0, np.frexp(amax)[1] - 1 + 127, 0) - down, 1)
    scale = np.exp2(byte - 127.0)
    codes = (blocks / scale).astype(np.float32).astype(dtype).astype(np.float64)
    return np.moveaxis((codes * scale).reshape(v.shape), -1, axis)


WIDE = False


def mx_kscale(k):
    if not WIDE:
        return np.ones(k)
    levels = np.array([10, -10, 5, -5, 0])
    if k % 512:
        return np.exp2(np.random.permutation(np.resize(levels, k // 32))).repeat(32)
    a = np.empty((k // 512, 16))
    for p in range(k // 512):
        a[p, :8] = np.random.permutation(np.resize(levels, 8))
        for g in range(8):
            far = levels[np.abs(levels - a[p, g]) >= 10]
            a[p, g + 8] = far[np.random.randint(len(far))]
    return np.exp2(a.ravel()).repeat(32)


def f64(x):
    return np.asarray(x).astype(np.float64)


def striped8(idx):
    return np.asarray(idx).reshape(8, -1, 16).transpose(0, 2, 1).reshape(128, -1).astype(np.uint16)


def unstriped8(offs):
    return offs.reshape(8, 16, -1).transpose(0, 2, 1).reshape(8, -1).astype(np.int64)


def pick8(x, idx, run):
    r = np.arange(len(x))
    return x[r[:, None], idx[r % (8 * run) // run]]


E2M1 = np.array([0.0, 0.5, 1.0, 1.5, 2.0, 3.0, 4.0, 6.0, -0.0, -0.5, -1.0, -1.5, -2.0, -3.0, -4.0, -6.0])


def pack_weight(w, fmt):
    k, n = w.shape
    w = f64(np.asarray(w, np.float32).astype(ml_dtypes.bfloat16)).reshape(k // 32, 32, n)
    amax = np.abs(w).max(1)
    if fmt == "e4m3":
        byte = np.frexp(amax)[1] - 1 + 127 - 7
    else:
        mant, ex = np.frexp(amax / 6.0)
        byte = np.where(mant > 0.5, ex, ex - 1) + 127
    byte = np.clip(np.where(amax > 0, byte, 1), 1, 254)
    scaled = (w * np.exp2(127.0 - byte)[:, None, :]).reshape(k, n).astype(np.float32)
    by_word = np.ascontiguousarray(scaled.reshape(k // 512, 128, 4, n).transpose(0, 1, 3, 2))
    if fmt == "e4m3":
        words = by_word.astype(ml_dtypes.float8_e4m3fn).view(np.uint8)
    else:
        c = by_word.astype(ml_dtypes.float4_e2m1fn).view(np.uint8) & 0xF
        words = (c[..., 0::2] | (c[..., 1::2] << 4)).reshape(k // 512, 128, 2 * n)
    return np.ascontiguousarray(words), np.ascontiguousarray(byte.astype(np.uint8).reshape(k // 512, 16, n))


def unpack_weight(words, scales, fmt):
    g, _, n = scales.shape
    words = np.ascontiguousarray(words).reshape(g, 128, n, -1)
    if fmt == "e4m3":
        vals = words.view(ml_dtypes.float8_e4m3fn).astype(np.float64)
    else:
        nib = np.empty((g, 128, n, 4), np.uint8)
        nib[..., 0::2] = words & 0xF
        nib[..., 1::2] = words >> 4
        vals = E2M1[nib]
    vals = vals * np.repeat(np.exp2(scales.astype(np.float64) - 127.0), 8, axis=1)[..., None]
    return vals.transpose(0, 1, 3, 2).reshape(g * 512, n)


D, E, T, Q, I = 512, 512, 1024, 128, 256


def setup_inputs():
    n = np.random.standard_normal
    idx = np.stack([np.random.permutation(T)[:I] for _ in range(8)])
    fd = mx_kscale(D)
    fe = mx_kscale(E)
    keysp = pack_weight(n((D, T)) / fd[:, None], "e2m1")
    return {
        "query": (n((D, Q)) * 0.6 / np.sqrt(D) * fd[:, None]).astype(np.float32),
        "keys_words": keysp[0],
        "keys_scales": keysp[1],
        "gout": (n((E, Q)) * 1 / np.sqrt(E) * fe[:, None]).astype(np.float32),
        "vals": (n((E, T)) / fe[:, None]).astype(np.float32),
        "offs": striped8(idx),
    }


def reference(query, keys_words, keys_scales, gout, vals, offs):
    idx = unstriped8(offs)
    keysu = unpack_weight(keys_words, keys_scales, "e2m1")
    queryq = mxq(f64(query), 0, "e4m3")
    a = queryq.T @ keysu
    goutq = mxq(f64(gout), 0, "e4m3")
    valsq = mxq(f64(vals), 0, "e4m3")
    dw = goutq.T @ valsq
    m1 = np.max(a, axis=1, keepdims=True)
    p = np.exp(a - m1)
    pk = np.exp(pick8(a, idx, 16) - m1)
    pf = np.zeros((Q, T))
    pf[np.arange(Q)[:, None], idx[np.arange(Q) % 128 // 16]] = pk
    z = np.sum(p, axis=1, keepdims=True)
    z2 = z - np.sum(pk, axis=1, keepdims=True)
    r = p / z
    u = (p - pf) / z2
    y = (r * (dw - np.sum(r * dw, axis=1, keepdims=True)) - u * (dw - np.sum(u * dw, axis=1, keepdims=True))) * 1024.0
    return y

@@ -1,0 +1,199 @@
+from contextlib import ExitStack
+
+import concourse.mybir as mybir
+
+F32 = mybir.dt.float32
+BF16 = mybir.dt.bfloat16
+I32 = mybir.dt.int32
+U32 = mybir.dt.uint32
+U16 = mybir.dt.uint16
+U8 = mybir.dt.uint8
+FP8X4 = mybir.dt.float8_e4m3fn_x4
+FP4X4 = mybir.dt.float4_e2m1fn_x4
+ALU = mybir.AluOpType
+ACT = mybir.ActivationFunctionType
+
+P = 128
+PACK = 4
+K = 512
+T = 1024
+Q = 128
+SLOTS = 256
+BANK = 512
+CHUNK = 256
+OUT_SCALE = 1024.0
+
+FLOPS = 2 * 2 * K * Q * T
+
+
+def interleave(copy, grouped, raw):
+    copy(
+        out=grouped.rearrange("p (c i) j -> p c j i", i=4),
+        in_=raw.rearrange("p j (c i) -> p c j i", i=4),
+    )
+
+
+def tile_attend_gknockout_heads_kernel(tc, query, keys_words, keys_scales, gout, vals, offs, out):
+    nc = tc.nc
+    chunks = T // CHUNK
+    with ExitStack() as ctx:
+        sb = ctx.enter_context(tc.tile_pool(name="sb", bufs=1))
+        ps = ctx.enter_context(tc.psum_pool(name="ps", bufs=1))
+
+        offsets = sb.tile([P, SLOTS // 16], U16, name="offsets")
+        q_raw = sb.tile([P, PACK, Q], F32, name="q_raw")
+        g_raw = sb.tile([P, PACK, Q], F32, name="g_raw")
+        k_words = sb.tile([P, 2 * T], U8, name="k_words", align_bytes=64)
+        k_scales = sb.tile([P, T], U8, name="k_scales", align_bytes=64)
+        v_raw = [sb.tile([P, PACK, CHUNK], F32, name="v_raw%d" % c) for c in range(chunks)]
+        vals_rows = vals.rearrange("(p j) t -> p j t", j=PACK)
+
+        nc.sync.dma_start(out=q_raw[:], in_=query.rearrange("(p j) q -> p j q", j=PACK))
+        nc.sync.dma_start(out=k_words[:].bitcast(I32), in_=keys_words[0].bitcast(I32))
+        for quad in range(4):
+            nc.sync.dma_start(
+                out=k_scales[32 * quad : 32 * quad + 4, :].bitcast(I32),
+                in_=keys_scales[0, 4 * quad : 4 * quad + 4, :].bitcast(I32),
+            )
+        nc.sync.dma_start(out=v_raw[0][:], in_=vals_rows[:, :, 0:CHUNK])
+        nc.sync.dma_start(out=g_raw[:], in_=gout.rearrange("(p j) q -> p j q", j=PACK))
+        nc.sync.dma_start(offsets[:], offs)
+        for c in range(1, chunks):
+            nc.sync.dma_start(out=v_raw[c][:], in_=vals_rows[:, :, c * CHUNK : (c + 1) * CHUNK])
+
+        pf = sb.tile([P, T], F32, name="pf")
+        nc.vector.memset(pf[:], 0.0)
+
+        def quantise(grouped, width, name):
+            codes = sb.tile([P, width], U32, name=name + "_codes", align_bytes=64)
+            scales = sb.tile([P, width], U8, name=name + "_scales", align_bytes=64)
+            nc.vector.quantize_mx(
+                out=codes[:].bitcast(FP8X4), scales=scales[:], in_=grouped[:].rearrange("p w j -> p (w j)")
+            )
+            return codes, scales
+
+        q_grp = sb.tile([P, Q, PACK], BF16, name="q_grp", align_bytes=64)
+        interleave(nc.vector.tensor_copy, q_grp[:], q_raw[:])
+        q_codes, q_scales = quantise(q_grp, Q, "q")
+
+        a = sb.tile([P, T], F32, name="a")
+        half_max = sb.tile([P, T // BANK], F32, name="half_max")
+        for h in range(T // BANK):
+            cols = slice(h * BANK, (h + 1) * BANK)
+            a_ps = ps.tile([P, BANK], F32, name="a_ps%d" % h)
+            nc.tensor.matmul_mx(
+                out=a_ps[:],
+                lhsT=q_codes[:].bitcast(FP8X4),
+                lhsT_scale=q_scales[:],
+                rhs=k_words[:, 2 * h * BANK : 2 * (h + 1) * BANK].bitcast(FP4X4),
+                rhs_scale=k_scales[:, cols],
+                start=True,
+                stop=True,
+            )
+            nc.vector.tensor_scalar(
+                out=a[:, cols], in0=a_ps[:], scalar1=1.0, scalar2=None, op0=ALU.mult, op1=ALU.max,
+                accum_out=half_max[:, h : h + 1],
+            )
+        neg_max = sb.tile([P, 1], F32, name="neg_max")
+        nc.vector.tensor_reduce(out=neg_max[:], in_=half_max[:], axis=mybir.AxisListType.X, op=ALU.max, negate=True)
+
+        g_grp = sb.tile([P, Q, PACK], BF16, name="g_grp", align_bytes=64)
+        interleave(nc.vector.tensor_copy, g_grp[:], g_raw[:])
+        g_codes, g_scales = quantise(g_grp, Q, "g")
+
+        v_grp = [sb.tile([P, CHUNK, PACK], BF16, name="v_grp%d" % c, align_bytes=64) for c in range(chunks)]
+
+        def interleave_vals(c):
+            for s in range(0, CHUNK, 128):
+                interleave(nc.scalar.copy, v_grp[c][:, s : s + 128, :], v_raw[c][:, :, s : s + 128])
+
+        interleave_vals(0)
+
+        pk = sb.tile([P, SLOTS], F32, name="pk")
+        pk_sum = sb.tile([P, 1], F32, name="pk_sum")
+        a_listed = sb.tile([P, SLOTS], F32, name="a_listed")
+        nc.vector.tensor_copy(out=a_listed[:], in_=a[:].indirect(offsets[:]))
+        nc.scalar.activation(out=pk[:], in_=a_listed[:], func=ACT.Exp, bias=neg_max[:], accum_out=pk_sum[:])
+        nc.vector.tensor_copy(out=pf[:].indirect(offsets[:]), in_=pk[:])
+        p = sb.tile([P, T], F32, name="p")
+        z_pair = sb.tile([P, 2], F32, name="z_pair")
+        nc.scalar.activation(out=p[:], in_=a[:], func=ACT.Exp, bias=neg_max[:], accum_out=z_pair[:, 0:1])
+
+        for c in range(1, chunks):
+            interleave_vals(c)
+
+        nc.vector.tensor_tensor(out=z_pair[:, 1:2], in0=z_pair[:, 0:1], in1=pk_sum[:], op=ALU.subtract)
+        inv_pair = sb.tile([P, 2], F32, name="inv_pair")
+        nc.vector.reciprocal(out=inv_pair[:], in_=z_pair[:])
+        share = sb.tile([P, 1], F32, name="share")
+        nc.vector.tensor_tensor(out=share[:], in0=pk_sum[:], in1=inv_pair[:, 0:1], op=ALU.mult)
+        gain_pair = sb.tile([P, 2], F32, name="gain_pair")
+        nc.vector.tensor_scalar(
+            out=gain_pair[:], in0=inv_pair[:], scalar1=OUT_SCALE, scalar2=None, op0=ALU.mult
+        )
+        diff = sb.tile([P, T], F32, name="diff")
+        nc.vector.scalar_tensor_tensor(
+            out=diff[:], in0=p[:], scalar=share[:], in1=pf[:], op0=ALU.mult, op1=ALU.subtract
+        )
+
+        sums = sb.tile([P, 2 * chunks], F32, name="sums")
+        r_dw = sb.tile([P, T], F32, name="r_dw")
+        diff_dw = sb.tile([P, T], F32, name="diff_dw")
+        for c in range(chunks):
+            cols = slice(c * CHUNK, (c + 1) * CHUNK)
+            v_codes, v_scales = quantise(v_grp[c], CHUNK, "v%d" % c)
+            dw_ps = ps.tile([P, CHUNK], F32, name="dw_ps%d" % c)
+            nc.tensor.matmul_mx(
+                out=dw_ps[:],
+                lhsT=g_codes[:].bitcast(FP8X4),
+                lhsT_scale=g_scales[:],
+                rhs=v_codes[:].bitcast(FP8X4),
+                rhs_scale=v_scales[:],
+                start=True,
+                stop=True,
+            )
+            nc.vector.scalar_tensor_tensor(
+                out=r_dw[:, cols], in0=dw_ps[:], scalar=gain_pair[:, 0:1], in1=p[:, cols],
+                op0=ALU.mult, op1=ALU.mult, accum_out=sums[:, c : c + 1],
+            )
+            nc.vector.scalar_tensor_tensor(
+                out=diff_dw[:, cols], in0=dw_ps[:], scalar=gain_pair[:, 1:2], in1=diff[:, cols],
+                op0=ALU.mult, op1=ALU.mult, accum_out=sums[:, chunks + c : chunks + c + 1],
+            )
+
+        p_gain = sb.tile([P, 1], F32, name="p_gain")
+        p_parts = sb.tile([P, chunks], F32, name="p_parts")
+        nc.vector.tensor_scalar(
+            out=p_parts[:], in0=sums[:, chunks:], scalar1=inv_pair[:, 0:1], scalar2=None,
+            op0=ALU.mult, op1=ALU.add, accum_out=p_gain[:],
+        )
+        diff_gain = sb.tile([P, 1], F32, name="diff_gain")
+        diff_parts = sb.tile([P, 2 * chunks], F32, name="diff_parts")
+        nc.vector.tensor_scalar(
+            out=diff_parts[:], in0=sums[:], scalar1=inv_pair[:, 1:2], scalar2=None,
+            op0=ALU.mult, op1=ALU.add, accum_out=diff_gain[:],
+        )
+
+        part = sb.tile([P, T], F32, name="part")
+        result = sb.tile([P, T], F32, name="result")
+
+        def first_terms(c):
+            cols = slice(c * CHUNK, (c + 1) * CHUNK)
+            nc.vector.scalar_tensor_tensor(
+                out=part[:, cols], in0=p[:, cols], scalar=p_gain[:], in1=diff_dw[:, cols],
+                op0=ALU.mult, op1=ALU.subtract,
+            )
+
+        def last_term(c):
+            cols = slice(c * CHUNK, (c + 1) * CHUNK)
+            nc.vector.scalar_tensor_tensor(
+                out=result[:, cols], in0=diff[:, cols], scalar=diff_gain[:], in1=part[:, cols],
+                op0=ALU.mult, op1=ALU.add,
+            )
+            nc.sync.dma_start(out=out[:, cols], in_=result[:, cols])
+
+        first_terms(0)
+        for c in range(1, chunks):
+            first_terms(c)
+            last_term(c - 1)
+        last_term(chunks - 1)

@@ -55,8 +55,8 @@ def tile_attend_gknockout_heads_kernel(tc, query, keys_words, keys_scales, gout,
                 out=k_scales[32 * quad : 32 * quad + 4, :].bitcast(I32),
                 in_=keys_scales[0, 4 * quad : 4 * quad + 4, :].bitcast(I32),
             )
-        nc.sync.dma_start(out=v_raw[0][:], in_=vals_rows[:, :, 0:CHUNK])
         nc.sync.dma_start(out=g_raw[:], in_=gout.rearrange("(p j) q -> p j q", j=PACK))
+        nc.sync.dma_start(out=v_raw[0][:], in_=vals_rows[:, :, 0:CHUNK])
         nc.sync.dma_start(offsets[:], offs)
         for c in range(1, chunks):
             nc.sync.dma_start(out=v_raw[c][:], in_=vals_rows[:, :, c * CHUNK : (c + 1) * CHUNK])
@@ -113,16 +113,25 @@ def tile_attend_gknockout_heads_kernel(tc, query, keys_words, keys_scales, gout,
         pk_sum = sb.tile([P, 1], F32, name="pk_sum")
         a_listed = sb.tile([P, SLOTS], F32, name="a_listed")
         nc.vector.tensor_copy(out=a_listed[:], in_=a[:].indirect(offsets[:]))
+        p = sb.tile([P, T], F32, name="p")
+        half_z = sb.tile([P, T // BANK], F32, name="half_z")
+        z_pair = sb.tile([P, 2], F32, name="z_pair")
+        nc.scalar.activation(
+            out=p[:, :BANK], in_=a[:, :BANK], func=ACT.Exp, bias=neg_max[:], accum_out=half_z[:, 0:1]
+        )
         nc.scalar.activation(out=pk[:], in_=a_listed[:], func=ACT.Exp, bias=neg_max[:], accum_out=pk_sum[:])
         nc.vector.tensor_copy(out=pf[:].indirect(offsets[:]), in_=pk[:])
-        p = sb.tile([P, T], F32, name="p")
-        z_pair = sb.tile([P, 2], F32, name="z_pair")
-        nc.scalar.activation(out=p[:], in_=a[:], func=ACT.Exp, bias=neg_max[:], accum_out=z_pair[:, 0:1])
+        nc.scalar.activation(
+            out=p[:, BANK:], in_=a[:, BANK:], func=ACT.Exp, bias=neg_max[:], accum_out=half_z[:, 1:2]
+        )
+        rest = sb.tile([P, 1], F32, name="rest")
+        nc.scalar.activation(out=rest[:], in_=pk_sum[:], func=ACT.Identity, scale=-1.0, bias=half_z[:, 0:1])
+        nc.scalar.activation(out=z_pair[:, 0:1], in_=half_z[:, 0:1], func=ACT.Identity, bias=half_z[:, 1:2])
+        nc.scalar.activation(out=z_pair[:, 1:2], in_=rest[:], func=ACT.Identity, bias=half_z[:, 1:2])
 
         for c in range(1, chunks):
             interleave_vals(c)
 
-        nc.vector.tensor_tensor(out=z_pair[:, 1:2], in0=z_pair[:, 0:1], in1=pk_sum[:], op=ALU.subtract)
         inv_pair = sb.tile([P, 2], F32, name="inv_pair")
         nc.vector.reciprocal(out=inv_pair[:], in_=z_pair[:])
         share = sb.tile([P, 1], F32, name="share")
@@ -136,15 +145,12 @@ def tile_attend_gknockout_heads_kernel(tc, query, keys_words, keys_scales, gout,
             out=diff[:], in0=p[:], scalar=share[:], in1=pf[:], op0=ALU.mult, op1=ALU.subtract
         )
 
-        sums = sb.tile([P, 2 * chunks], F32, name="sums")
-        r_dw = sb.tile([P, T], F32, name="r_dw")
-        diff_dw = sb.tile([P, T], F32, name="diff_dw")
+        dw_banks = [ps.tile([P, BANK], F32, name="dw_ps%d" % h) for h in range(T // BANK)]
         for c in range(chunks):
-            cols = slice(c * CHUNK, (c + 1) * CHUNK)
             v_codes, v_scales = quantise(v_grp[c], CHUNK, "v%d" % c)
-            dw_ps = ps.tile([P, CHUNK], F32, name="dw_ps%d" % c)
+            h, first = divmod(c * CHUNK, BANK)
             nc.tensor.matmul_mx(
-                out=dw_ps[:],
+                out=dw_banks[h][:, first : first + CHUNK],
                 lhsT=g_codes[:].bitcast(FP8X4),
                 lhsT_scale=g_scales[:],
                 rhs=v_codes[:].bitcast(FP8X4),
@@ -152,26 +158,43 @@ def tile_attend_gknockout_heads_kernel(tc, query, keys_words, keys_scales, gout,
                 start=True,
                 stop=True,
             )
+
+        spare = [v_grp[c][:].rearrange("p w j -> p (w j)").bitcast(F32) for c in range(chunks)]
+        r_sums = sb.tile([P, 2], F32, name="r_sums")
+        diff_sums = sb.tile([P, 2], F32, name="diff_sums")
+        diff_dw = [spare[3], spare[1]]
+
+        def r_pass(h):
             nc.vector.scalar_tensor_tensor(
-                out=r_dw[:, cols], in0=dw_ps[:], scalar=gain_pair[:, 0:1], in1=p[:, cols],
-                op0=ALU.mult, op1=ALU.mult, accum_out=sums[:, c : c + 1],
-            )
-            nc.vector.scalar_tensor_tensor(
-                out=diff_dw[:, cols], in0=dw_ps[:], scalar=gain_pair[:, 1:2], in1=diff[:, cols],
-                op0=ALU.mult, op1=ALU.mult, accum_out=sums[:, chunks + c : chunks + c + 1],
+                out=spare[2 - 2 * h], in0=dw_banks[h][:], scalar=gain_pair[:, 0:1], in1=p[:, h * BANK : (h + 1) * BANK],
+                op0=ALU.mult, op1=ALU.mult, accum_out=r_sums[:, h : h + 1],
             )
 
+        def diff_pass(h):
+            nc.vector.scalar_tensor_tensor(
+                out=diff_dw[h], in0=dw_banks[h][:], scalar=gain_pair[:, 1:2], in1=diff[:, h * BANK : (h + 1) * BANK],
+                op0=ALU.mult, op1=ALU.mult, accum_out=diff_sums[:, h : h + 1],
+            )
+
+        r_pass(0)
+        diff_pass(0)
+        diff_pass(1)
+        r_pass(1)
+
         p_gain = sb.tile([P, 1], F32, name="p_gain")
-        p_parts = sb.tile([P, chunks], F32, name="p_parts")
         nc.vector.tensor_scalar(
-            out=p_parts[:], in0=sums[:, chunks:], scalar1=inv_pair[:, 0:1], scalar2=None,
-            op0=ALU.mult, op1=ALU.add, accum_out=p_gain[:],
+            out=p_gain[:], in0=diff_sums[:, 0:1], scalar1=diff_sums[:, 1:2], scalar2=inv_pair[:, 0:1],
+            op0=ALU.add, op1=ALU.mult,
+        )
+        three_sums = sb.tile([P, 1], F32, name="three_sums")
+        nc.vector.tensor_scalar(
+            out=three_sums[:], in0=diff_sums[:, 0:1], scalar1=diff_sums[:, 1:2], scalar2=r_sums[:, 0:1],
+            op0=ALU.add, op1=ALU.add,
         )
         diff_gain = sb.tile([P, 1], F32, name="diff_gain")
-        diff_parts = sb.tile([P, 2 * chunks], F32, name="diff_parts")
         nc.vector.tensor_scalar(
-            out=diff_parts[:], in0=sums[:], scalar1=inv_pair[:, 1:2], scalar2=None,
-            op0=ALU.mult, op1=ALU.add, accum_out=diff_gain[:],
+            out=diff_gain[:], in0=r_sums[:, 1:2], scalar1=three_sums[:], scalar2=inv_pair[:, 1:2],
+            op0=ALU.add, op1=ALU.mult,
         )
 
         part = sb.tile([P, T], F32, name="part")
@@ -180,7 +203,7 @@ def tile_attend_gknockout_heads_kernel(tc, query, keys_words, keys_scales, gout,
         def first_terms(c):
             cols = slice(c * CHUNK, (c + 1) * CHUNK)
             nc.vector.scalar_tensor_tensor(
-                out=part[:, cols], in0=p[:, cols], scalar=p_gain[:], in1=diff_dw[:, cols],
+                out=part[:, cols], in0=p[:, cols], scalar=p_gain[:], in1=diff_dw[c * CHUNK // BANK][:, c * CHUNK % BANK : c * CHUNK % BANK + CHUNK],
                 op0=ALU.mult, op1=ALU.subtract,
             )
 

@@ -22,6 +22,9 @@ SLOTS = 256
 BANK = 512
 CHUNK = 256
 OUT_SCALE = 1024.0
+EXP_FIRST = 256
+LOADS = (0, 384, 768, T)
+PIECE = 128
 
 FLOPS = 2 * 2 * K * Q * T
 
@@ -45,7 +48,11 @@ def tile_attend_gknockout_heads_kernel(tc, query, keys_words, keys_scales, gout,
         g_raw = sb.tile([P, PACK, Q], F32, name="g_raw")
         k_words = sb.tile([P, 2 * T], U8, name="k_words", align_bytes=64)
         k_scales = sb.tile([P, T], U8, name="k_scales", align_bytes=64)
-        v_raw = [sb.tile([P, PACK, CHUNK], F32, name="v_raw%d" % c) for c in range(chunks)]
+        first = sb.tile([P, PACK * LOADS[1]], F32, name="first")
+        v_raw = [first[:].rearrange("p (j t) -> p j t", j=PACK)]
+        v_raw.extend(
+            sb.tile([P, PACK, hi - lo], F32, name="v_raw%d" % lo)[:] for lo, hi in zip(LOADS[1:-1], LOADS[2:])
+        )
         vals_rows = vals.rearrange("(p j) t -> p j t", j=PACK)
 
         nc.sync.dma_start(out=q_raw[:], in_=query.rearrange("(p j) q -> p j q", j=PACK))
@@ -55,11 +62,11 @@ def tile_attend_gknockout_heads_kernel(tc, query, keys_words, keys_scales, gout,
                 out=k_scales[32 * quad : 32 * quad + 4, :].bitcast(I32),
                 in_=keys_scales[0, 4 * quad : 4 * quad + 4, :].bitcast(I32),
             )
-        nc.sync.dma_start(out=g_raw[:], in_=gout.rearrange("(p j) q -> p j q", j=PACK))
-        nc.sync.dma_start(out=v_raw[0][:], in_=vals_rows[:, :, 0:CHUNK])
         nc.sync.dma_start(offsets[:], offs)
-        for c in range(1, chunks):
-            nc.sync.dma_start(out=v_raw[c][:], in_=vals_rows[:, :, c * CHUNK : (c + 1) * CHUNK])
+        nc.sync.dma_start(out=v_raw[0], in_=vals_rows[:, :, : LOADS[1]])
+        nc.sync.dma_start(out=g_raw[:], in_=gout.rearrange("(p j) q -> p j q", j=PACK))
+        for n in range(1, len(v_raw)):
+            nc.sync.dma_start(out=v_raw[n], in_=vals_rows[:, :, LOADS[n] : LOADS[n + 1]])
 
         pf = sb.tile([P, T], F32, name="pf")
         nc.vector.memset(pf[:], 0.0)
@@ -68,13 +75,13 @@ def tile_attend_gknockout_heads_kernel(tc, query, keys_words, keys_scales, gout,
             codes = sb.tile([P, width], U32, name=name + "_codes", align_bytes=64)
             scales = sb.tile([P, width], U8, name=name + "_scales", align_bytes=64)
             nc.vector.quantize_mx(
-                out=codes[:].bitcast(FP8X4), scales=scales[:], in_=grouped[:].rearrange("p w j -> p (w j)")
+                out=codes[:].bitcast(FP8X4), scales=scales[:], in_=grouped.rearrange("p w j -> p (w j)")
             )
             return codes, scales
 
         q_grp = sb.tile([P, Q, PACK], BF16, name="q_grp", align_bytes=64)
         interleave(nc.vector.tensor_copy, q_grp[:], q_raw[:])
-        q_codes, q_scales = quantise(q_grp, Q, "q")
+        q_codes, q_scales = quantise(q_grp[:], Q, "q")
 
         a = sb.tile([P, T], F32, name="a")
         half_max = sb.tile([P, T // BANK], F32, name="half_max")
@@ -94,43 +101,54 @@ def tile_attend_gknockout_heads_kernel(tc, query, keys_words, keys_scales, gout,
                 out=a[:, cols], in0=a_ps[:], scalar1=1.0, scalar2=None, op0=ALU.mult, op1=ALU.max,
                 accum_out=half_max[:, h : h + 1],
             )
-        neg_max = sb.tile([P, 1], F32, name="neg_max")
-        nc.vector.tensor_reduce(out=neg_max[:], in_=half_max[:], axis=mybir.AxisListType.X, op=ALU.max, negate=True)
+
+        neg_max = sb.tile([P, 1], F32, name="neg_max")[:]
+        nc.vector.tensor_reduce(out=neg_max, in_=half_max[:], axis=mybir.AxisListType.X, op=ALU.max, negate=True)
 
         g_grp = sb.tile([P, Q, PACK], BF16, name="g_grp", align_bytes=64)
-        interleave(nc.vector.tensor_copy, g_grp[:], g_raw[:])
-        g_codes, g_scales = quantise(g_grp, Q, "g")
+        nc.gpsimd.tensor_scalar(
+            out=g_grp[:], in0=g_raw[:].rearrange("p j q -> p q j"), scalar1=1.0, scalar2=0.0,
+            op0=ALU.mult, op1=ALU.add,
+        )
 
-        v_grp = [sb.tile([P, CHUNK, PACK], BF16, name="v_grp%d" % c, align_bytes=64) for c in range(chunks)]
+        diff = sb.tile([P, T], F32, name="diff", align_bytes=64)
+        late = sb.tile([P, T], F32, name="late", align_bytes=64)
+        v_grp = [
+            tile[:, lo : lo + BANK].bitcast(BF16).rearrange("p (w j) -> p w j", j=PACK)
+            for tile in (diff, late)
+            for lo in (0, BANK)
+        ]
 
-        def interleave_vals(c):
-            for s in range(0, CHUNK, 128):
-                interleave(nc.scalar.copy, v_grp[c][:, s : s + 128, :], v_raw[c][:, :, s : s + 128])
+        def interleave_vals(n):
+            for t in range(LOADS[n], LOADS[n + 1], PIECE):
+                c, s = divmod(t, CHUNK)
+                lo = t - LOADS[n]
+                interleave(nc.scalar.copy, v_grp[c][:, s : s + PIECE, :], v_raw[n][:, :, lo : lo + PIECE])
 
         interleave_vals(0)
 
-        pk = sb.tile([P, SLOTS], F32, name="pk")
+        pk = first[:, 3 * LOADS[1] : 3 * LOADS[1] + SLOTS]
         pk_sum = sb.tile([P, 1], F32, name="pk_sum")
-        a_listed = sb.tile([P, SLOTS], F32, name="a_listed")
-        nc.vector.tensor_copy(out=a_listed[:], in_=a[:].indirect(offsets[:]))
-        p = sb.tile([P, T], F32, name="p")
+        a_listed = diff[:, T - SLOTS :]
+        nc.vector.tensor_copy(out=a_listed, in_=a[:].indirect(offsets[:]))
+        p = first[:, :T]
         half_z = sb.tile([P, T // BANK], F32, name="half_z")
         z_pair = sb.tile([P, 2], F32, name="z_pair")
         nc.scalar.activation(
-            out=p[:, :BANK], in_=a[:, :BANK], func=ACT.Exp, bias=neg_max[:], accum_out=half_z[:, 0:1]
+            out=p[:, :EXP_FIRST], in_=a[:, :EXP_FIRST], func=ACT.Exp, bias=neg_max, accum_out=half_z[:, 0:1]
         )
-        nc.scalar.activation(out=pk[:], in_=a_listed[:], func=ACT.Exp, bias=neg_max[:], accum_out=pk_sum[:])
-        nc.vector.tensor_copy(out=pf[:].indirect(offsets[:]), in_=pk[:])
+        nc.scalar.activation(out=pk, in_=a_listed, func=ACT.Exp, bias=neg_max, accum_out=pk_sum[:])
+        nc.vector.tensor_copy(out=pf[:].indirect(offsets[:]), in_=pk)
         nc.scalar.activation(
-            out=p[:, BANK:], in_=a[:, BANK:], func=ACT.Exp, bias=neg_max[:], accum_out=half_z[:, 1:2]
+            out=p[:, EXP_FIRST:], in_=a[:, EXP_FIRST:], func=ACT.Exp, bias=neg_max, accum_out=half_z[:, 1:2]
         )
         rest = sb.tile([P, 1], F32, name="rest")
         nc.scalar.activation(out=rest[:], in_=pk_sum[:], func=ACT.Identity, scale=-1.0, bias=half_z[:, 0:1])
         nc.scalar.activation(out=z_pair[:, 0:1], in_=half_z[:, 0:1], func=ACT.Identity, bias=half_z[:, 1:2])
         nc.scalar.activation(out=z_pair[:, 1:2], in_=rest[:], func=ACT.Identity, bias=half_z[:, 1:2])
 
-        for c in range(1, chunks):
-            interleave_vals(c)
+        for n in range(1, len(v_raw)):
+            interleave_vals(n)
 
         inv_pair = sb.tile([P, 2], F32, name="inv_pair")
         nc.vector.reciprocal(out=inv_pair[:], in_=z_pair[:])
@@ -140,11 +158,8 @@ def tile_attend_gknockout_heads_kernel(tc, query, keys_words, keys_scales, gout,
         nc.vector.tensor_scalar(
             out=gain_pair[:], in0=inv_pair[:], scalar1=OUT_SCALE, scalar2=None, op0=ALU.mult
         )
-        diff = sb.tile([P, T], F32, name="diff")
-        nc.vector.scalar_tensor_tensor(
-            out=diff[:], in0=p[:], scalar=share[:], in1=pf[:], op0=ALU.mult, op1=ALU.subtract
-        )
 
+        g_codes, g_scales = quantise(g_grp[:], Q, "g")
         dw_banks = [ps.tile([P, BANK], F32, name="dw_ps%d" % h) for h in range(T // BANK)]
         for c in range(chunks):
             v_codes, v_scales = quantise(v_grp[c], CHUNK, "v%d" % c)
@@ -159,14 +174,18 @@ def tile_attend_gknockout_heads_kernel(tc, query, keys_words, keys_scales, gout,
                 stop=True,
             )
 
-        spare = [v_grp[c][:].rearrange("p w j -> p (w j)").bitcast(F32) for c in range(chunks)]
+        nc.vector.scalar_tensor_tensor(
+            out=diff[:], in0=p, scalar=share[:], in1=pf[:], op0=ALU.mult, op1=ALU.subtract
+        )
+        spare = sb.tile([P, T], F32, name="spare")
         r_sums = sb.tile([P, 2], F32, name="r_sums")
         diff_sums = sb.tile([P, 2], F32, name="diff_sums")
-        diff_dw = [spare[3], spare[1]]
+        diff_dw = [late[:, BANK:], spare[:, :BANK]]
+        r_dw = [late[:, :BANK], spare[:, BANK:]]
 
         def r_pass(h):
             nc.vector.scalar_tensor_tensor(
-                out=spare[2 - 2 * h], in0=dw_banks[h][:], scalar=gain_pair[:, 0:1], in1=p[:, h * BANK : (h + 1) * BANK],
+                out=r_dw[h], in0=dw_banks[h][:], scalar=gain_pair[:, 0:1], in1=p[:, h * BANK : (h + 1) * BANK],
                 op0=ALU.mult, op1=ALU.mult, accum_out=r_sums[:, h : h + 1],
             )
 
@@ -200,23 +219,22 @@ def tile_attend_gknockout_heads_kernel(tc, query, keys_words, keys_scales, gout,
         part = sb.tile([P, T], F32, name="part")
         result = sb.tile([P, T], F32, name="result")
 
-        def first_terms(c):
-            cols = slice(c * CHUNK, (c + 1) * CHUNK)
+        def first_terms(lo, hi):
+            h = lo // BANK
             nc.vector.scalar_tensor_tensor(
-                out=part[:, cols], in0=p[:, cols], scalar=p_gain[:], in1=diff_dw[c * CHUNK // BANK][:, c * CHUNK % BANK : c * CHUNK % BANK + CHUNK],
+                out=part[:, lo:hi], in0=p[:, lo:hi], scalar=p_gain[:], in1=diff_dw[h][:, lo - h * BANK : hi - h * BANK],
                 op0=ALU.mult, op1=ALU.subtract,
             )
 
-        def last_term(c):
-            cols = slice(c * CHUNK, (c + 1) * CHUNK)
+        def last_term(lo, hi):
             nc.vector.scalar_tensor_tensor(
-                out=result[:, cols], in0=diff[:, cols], scalar=diff_gain[:], in1=part[:, cols],
+                out=result[:, lo:hi], in0=diff[:, lo:hi], scalar=diff_gain[:], in1=part[:, lo:hi],
                 op0=ALU.mult, op1=ALU.add,
             )
-            nc.sync.dma_start(out=out[:, cols], in_=result[:, cols])
+            nc.sync.dma_start(out=out[:, lo:hi], in_=result[:, lo:hi])
 
-        first_terms(0)
-        for c in range(1, chunks):
-            first_terms(c)
-            last_term(c - 1)
-        last_term(chunks - 1)
+        first_terms(0, CHUNK)
+        for lo in range(CHUNK, T, CHUNK):
+            first_terms(lo, lo + CHUNK)
+            last_term(lo - CHUNK, lo)
+        last_term(T - CHUNK, T)

from contextlib import ExitStack

import concourse.mybir as mybir

F32 = mybir.dt.float32
BF16 = mybir.dt.bfloat16
I32 = mybir.dt.int32
U32 = mybir.dt.uint32
U16 = mybir.dt.uint16
U8 = mybir.dt.uint8
FP8X4 = mybir.dt.float8_e4m3fn_x4
FP4X4 = mybir.dt.float4_e2m1fn_x4
ALU = mybir.AluOpType
ACT = mybir.ActivationFunctionType

P = 128
PACK = 4
K = 512
T = 1024
Q = 128
SLOTS = 256
BANK = 512
CHUNK = 256
OUT_SCALE = 1024.0
EXP_FIRST = 256
LOADS = (0, 384, 768, T)
PIECE = 128

FLOPS = 2 * 2 * K * Q * T


def interleave(copy, grouped, raw):
    copy(
        out=grouped.rearrange("p (c i) j -> p c j i", i=4),
        in_=raw.rearrange("p j (c i) -> p c j i", i=4),
    )


def tile_attend_gknockout_heads_kernel(tc, query, keys_words, keys_scales, gout, vals, offs, out):
    nc = tc.nc
    chunks = T // CHUNK
    with ExitStack() as ctx:
        sb = ctx.enter_context(tc.tile_pool(name="sb", bufs=1))
        ps = ctx.enter_context(tc.psum_pool(name="ps", bufs=1))

        offsets = sb.tile([P, SLOTS // 16], U16, name="offsets")
        q_raw = sb.tile([P, PACK, Q], F32, name="q_raw")
        g_raw = sb.tile([P, PACK, Q], F32, name="g_raw")
        k_words = sb.tile([P, 2 * T], U8, name="k_words", align_bytes=64)
        k_scales = sb.tile([P, T], U8, name="k_scales", align_bytes=64)
        first = sb.tile([P, PACK * LOADS[1]], F32, name="first")
        v_raw = [first[:].rearrange("p (j t) -> p j t", j=PACK)]
        v_raw.extend(
            sb.tile([P, PACK, hi - lo], F32, name="v_raw%d" % lo)[:] for lo, hi in zip(LOADS[1:-1], LOADS[2:])
        )
        vals_rows = vals.rearrange("(p j) t -> p j t", j=PACK)

        nc.sync.dma_start(out=q_raw[:], in_=query.rearrange("(p j) q -> p j q", j=PACK))
        nc.sync.dma_start(out=k_words[:].bitcast(I32), in_=keys_words[0].bitcast(I32))
        for quad in range(4):
            nc.sync.dma_start(
                out=k_scales[32 * quad : 32 * quad + 4, :].bitcast(I32),
                in_=keys_scales[0, 4 * quad : 4 * quad + 4, :].bitcast(I32),
            )
        nc.sync.dma_start(offsets[:], offs)
        nc.sync.dma_start(out=v_raw[0], in_=vals_rows[:, :, : LOADS[1]])
        nc.sync.dma_start(out=g_raw[:], in_=gout.rearrange("(p j) q -> p j q", j=PACK))
        for n in range(1, len(v_raw)):
            nc.sync.dma_start(out=v_raw[n], in_=vals_rows[:, :, LOADS[n] : LOADS[n + 1]])

        pf = sb.tile([P, T], F32, name="pf")
        nc.vector.memset(pf[:], 0.0)

        def quantise(grouped, width, name):
            codes = sb.tile([P, width], U32, name=name + "_codes", align_bytes=64)
            scales = sb.tile([P, width], U8, name=name + "_scales", align_bytes=64)
            nc.vector.quantize_mx(
                out=codes[:].bitcast(FP8X4), scales=scales[:], in_=grouped.rearrange("p w j -> p (w j)")
            )
            return codes, scales

        q_grp = sb.tile([P, Q, PACK], BF16, name="q_grp", align_bytes=64)
        interleave(nc.vector.tensor_copy, q_grp[:], q_raw[:])
        q_codes, q_scales = quantise(q_grp[:], Q, "q")

        a = sb.tile([P, T], F32, name="a")
        half_max = sb.tile([P, T // BANK], F32, name="half_max")
        for h in range(T // BANK):
            cols = slice(h * BANK, (h + 1) * BANK)
            a_ps = ps.tile([P, BANK], F32, name="a_ps%d" % h)
            nc.tensor.matmul_mx(
                out=a_ps[:],
                lhsT=q_codes[:].bitcast(FP8X4),
                lhsT_scale=q_scales[:],
                rhs=k_words[:, 2 * h * BANK : 2 * (h + 1) * BANK].bitcast(FP4X4),
                rhs_scale=k_scales[:, cols],
                start=True,
                stop=True,
            )
            nc.vector.tensor_scalar(
                out=a[:, cols], in0=a_ps[:], scalar1=1.0, scalar2=None, op0=ALU.mult, op1=ALU.max,
                accum_out=half_max[:, h : h + 1],
            )

        neg_max = sb.tile([P, 1], F32, name="neg_max")[:]
        nc.vector.tensor_reduce(out=neg_max, in_=half_max[:], axis=mybir.AxisListType.X, op=ALU.max, negate=True)

        g_grp = sb.tile([P, Q, PACK], BF16, name="g_grp", align_bytes=64)
        nc.gpsimd.tensor_scalar(
            out=g_grp[:], in0=g_raw[:].rearrange("p j q -> p q j"), scalar1=1.0, scalar2=0.0,
            op0=ALU.mult, op1=ALU.add,
        )

        diff = sb.tile([P, T], F32, name="diff", align_bytes=64)
        late = sb.tile([P, T], F32, name="late", align_bytes=64)
        v_grp = [
            tile[:, lo : lo + BANK].bitcast(BF16).rearrange("p (w j) -> p w j", j=PACK)
            for tile in (diff, late)
            for lo in (0, BANK)
        ]

        def interleave_vals(n):
            for t in range(LOADS[n], LOADS[n + 1], PIECE):
                c, s = divmod(t, CHUNK)
                lo = t - LOADS[n]
                interleave(nc.scalar.copy, v_grp[c][:, s : s + PIECE, :], v_raw[n][:, :, lo : lo + PIECE])

        interleave_vals(0)

        pk = first[:, 3 * LOADS[1] : 3 * LOADS[1] + SLOTS]
        pk_sum = sb.tile([P, 1], F32, name="pk_sum")
        a_listed = diff[:, T - SLOTS :]
        nc.vector.tensor_copy(out=a_listed, in_=a[:].indirect(offsets[:]))
        p = first[:, :T]
        half_z = sb.tile([P, T // BANK], F32, name="half_z")
        z_pair = sb.tile([P, 2], F32, name="z_pair")
        nc.scalar.activation(
            out=p[:, :EXP_FIRST], in_=a[:, :EXP_FIRST], func=ACT.Exp, bias=neg_max, accum_out=half_z[:, 0:1]
        )
        nc.scalar.activation(out=pk, in_=a_listed, func=ACT.Exp, bias=neg_max, accum_out=pk_sum[:])
        nc.vector.tensor_copy(out=pf[:].indirect(offsets[:]), in_=pk)
        nc.scalar.activation(
            out=p[:, EXP_FIRST:], in_=a[:, EXP_FIRST:], func=ACT.Exp, bias=neg_max, accum_out=half_z[:, 1:2]
        )
        rest = sb.tile([P, 1], F32, name="rest")
        nc.scalar.activation(out=rest[:], in_=pk_sum[:], func=ACT.Identity, scale=-1.0, bias=half_z[:, 0:1])
        nc.scalar.activation(out=z_pair[:, 0:1], in_=half_z[:, 0:1], func=ACT.Identity, bias=half_z[:, 1:2])
        nc.scalar.activation(out=z_pair[:, 1:2], in_=rest[:], func=ACT.Identity, bias=half_z[:, 1:2])

        for n in range(1, len(v_raw)):
            interleave_vals(n)

        inv_pair = sb.tile([P, 2], F32, name="inv_pair")
        nc.vector.reciprocal(out=inv_pair[:], in_=z_pair[:])
        share = sb.tile([P, 1], F32, name="share")
        nc.vector.tensor_tensor(out=share[:], in0=pk_sum[:], in1=inv_pair[:, 0:1], op=ALU.mult)
        gain_pair = sb.tile([P, 2], F32, name="gain_pair")
        nc.vector.tensor_scalar(
            out=gain_pair[:], in0=inv_pair[:], scalar1=OUT_SCALE, scalar2=None, op0=ALU.mult
        )

        g_codes, g_scales = quantise(g_grp[:], Q, "g")
        dw_banks = [ps.tile([P, BANK], F32, name="dw_ps%d" % h) for h in range(T // BANK)]
        for c in range(chunks):
            v_codes, v_scales = quantise(v_grp[c], CHUNK, "v%d" % c)
            h, first = divmod(c * CHUNK, BANK)
            nc.tensor.matmul_mx(
                out=dw_banks[h][:, first : first + CHUNK],
                lhsT=g_codes[:].bitcast(FP8X4),
                lhsT_scale=g_scales[:],
                rhs=v_codes[:].bitcast(FP8X4),
                rhs_scale=v_scales[:],
                start=True,
                stop=True,
            )

        nc.vector.scalar_tensor_tensor(
            out=diff[:], in0=p, scalar=share[:], in1=pf[:], op0=ALU.mult, op1=ALU.subtract
        )
        spare = sb.tile([P, T], F32, name="spare")
        r_sums = sb.tile([P, 2], F32, name="r_sums")
        diff_sums = sb.tile([P, 2], F32, name="diff_sums")
        diff_dw = [late[:, BANK:], spare[:, :BANK]]
        r_dw = [late[:, :BANK], spare[:, BANK:]]

        def r_pass(h):
            nc.vector.scalar_tensor_tensor(
                out=r_dw[h], in0=dw_banks[h][:], scalar=gain_pair[:, 0:1], in1=p[:, h * BANK : (h + 1) * BANK],
                op0=ALU.mult, op1=ALU.mult, accum_out=r_sums[:, h : h + 1],
            )

        def diff_pass(h):
            nc.vector.scalar_tensor_tensor(
                out=diff_dw[h], in0=dw_banks[h][:], scalar=gain_pair[:, 1:2], in1=diff[:, h * BANK : (h + 1) * BANK],
                op0=ALU.mult, op1=ALU.mult, accum_out=diff_sums[:, h : h + 1],
            )

        r_pass(0)
        diff_pass(0)
        diff_pass(1)
        r_pass(1)

        p_gain = sb.tile([P, 1], F32, name="p_gain")
        nc.vector.tensor_scalar(
            out=p_gain[:], in0=diff_sums[:, 0:1], scalar1=diff_sums[:, 1:2], scalar2=inv_pair[:, 0:1],
            op0=ALU.add, op1=ALU.mult,
        )
        three_sums = sb.tile([P, 1], F32, name="three_sums")
        nc.vector.tensor_scalar(
            out=three_sums[:], in0=diff_sums[:, 0:1], scalar1=diff_sums[:, 1:2], scalar2=r_sums[:, 0:1],
            op0=ALU.add, op1=ALU.add,
        )
        diff_gain = sb.tile([P, 1], F32, name="diff_gain")
        nc.vector.tensor_scalar(
            out=diff_gain[:], in0=r_sums[:, 1:2], scalar1=three_sums[:], scalar2=inv_pair[:, 1:2],
            op0=ALU.add, op1=ALU.mult,
        )

        part = sb.tile([P, T], F32, name="part")
        result = sb.tile([P, T], F32, name="result")

        def first_terms(lo, hi):
            h = lo // BANK
            nc.vector.scalar_tensor_tensor(
                out=part[:, lo:hi], in0=p[:, lo:hi], scalar=p_gain[:], in1=diff_dw[h][:, lo - h * BANK : hi - h * BANK],
                op0=ALU.mult, op1=ALU.subtract,
            )

        def last_term(lo, hi):
            nc.vector.scalar_tensor_tensor(
                out=result[:, lo:hi], in0=diff[:, lo:hi], scalar=diff_gain[:], in1=part[:, lo:hi],
                op0=ALU.mult, op1=ALU.add,
            )
            nc.sync.dma_start(out=out[:, lo:hi], in_=result[:, lo:hi])

        first_terms(0, CHUNK)
        for lo in range(CHUNK, T, CHUNK):
            first_terms(lo, lo + CHUNK)
            last_term(lo - CHUNK, lo)
        last_term(T - CHUNK, T)
